import numpy as np, ml_dtypes
CORES = [9,25,41,57]
N = 4
BF = ml_dtypes.bfloat16
def f(rng, *shape):
    return (rng.standard_normal(shape, dtype=np.float32) * np.exp2(rng.integers(-2, 3, shape[:-1] + (1,)))).astype(BF)
def wide(rng, *shape):
    v = f(rng, *shape).astype(np.float32); k = shape[:-2] + (1, shape[-1])
    return (v * np.exp2(rng.integers(-6, 7, k)) * (rng.random(k) > 0.0625)).astype(BF)
def gentries(a):
    return np.ascontiguousarray(a.reshape(8, 16, -1).transpose(0, 2, 1)).reshape(8, -1)
def gtable(e):
    e = np.asarray(e); return np.ascontiguousarray(e.reshape(8, -1, 16).transpose(0, 2, 1)).reshape(128, -1).astype(np.int32)
H, C, M, W = 4096, 2048, 4, 1024
JM = 2.0 ** -12
def positive(v):
    return np.abs(v.astype(np.float32)).astype(BF)
def glists(e):
    return np.stack([gtable(v) for v in e])
def lastplaces(rng):
    c = np.sort(np.argsort(rng.random((N, 8, H - 1)), -1)[..., :C - 1], -1)
    return np.concatenate([c, np.full((N, 8, 1), H - 1)], -1)
def classes(e):
    return np.stack([np.stack([np.searchsorted(v, np.arange(H)) for v in u]) for u in e])
def setup_inputs(rng):
    e = lastplaces(rng)
    return {"w": positive(f(rng, N, 128, W)), "pm": glists(np.argsort(rng.random((N, 8, H)), -1)), "cl": glists(classes(e)), "en": glists(e),
            "al": rng.integers(0, 2 ** M, (N, 8, C)).astype(np.int32), "tg": rng.integers(0, 2, (N, 128, M)).astype(np.int32),
            "st": (0.5 + 0.5 * rng.random((N, 128, M))).astype(np.float32), "ju": (JM * rng.random((N, 128, M))).astype(np.float32), "mi": (0.25 + 0.75 * rng.random((N, 128, M))).astype(np.float32)}
def setup_inputs_runs(rng):
    d = setup_inputs(rng); b = rng.integers(0, C, (N, 8, 1)); b[:, 0] = 0; b[:, 1] = C - 1
    c = np.arange(C).reshape(1, 1, C); e = c + (H - C) * (c >= b); d["cl"] = glists(classes(e)); d["en"] = glists(e)
    p = np.argsort(rng.random((N, 8, H)), -1); p[:, 2] = np.arange(H); p[:, 3] = np.arange(H)[::-1]; d["pm"] = glists(p); return d
def setup_inputs_still(rng):
    d = setup_inputs(rng); m = rng.random((N, 1, M)) < 0.5; m[:, :, 0] = True
    d["st"] = np.where(m, np.float32(1), d["st"]); d["ju"] = np.where(m, np.float32(0), d["ju"])
    d["mi"] = np.where(rng.random((N, 128, M)) < 0.25, np.float32(1), d["mi"]); return d
def setup_inputs_sharp(rng):
    d = setup_inputs(rng); d["mi"] = np.full((N, 128, M), 0.25, np.float32)
    d["ju"] = np.where(rng.random((N, 128, M)) < 0.5, np.float32(JM), d["ju"]); d["st"] = np.where(rng.random((N, 128, M)) < 0.25, np.float32(0.5), d["st"])
    q = rng.integers(0, N); v = int(rng.integers(0, 2 ** M)); d["al"][q, 0] = v; z = (v >> np.arange(M)) & 1
    d["tg"][q, 0] = 1 - z; d["tg"][q, 1] = z; return d
def setup_inputs_few(rng):
    d = setup_inputs(rng); h = rng.integers(0, H, 128); h[0] = 0; h[127] = H - 1
    v = np.zeros((128, H), np.float32); v[np.arange(128), h] = 1 + 7 * rng.random(128)
    d["w"] = np.ascontiguousarray(v.reshape(128, N, W).transpose(1, 0, 2)).astype(BF); return d
def setup_inputs_spread(rng):
    d = setup_inputs(rng); d["w"] = positive(wide(rng, N, 128, W)); b = rng.random((N, 8, C, M)) < rng.random((N, 8, 1, M))
    d["al"] = np.sum(b * (1 << np.arange(M)), -1).astype(np.int32); return d
def check_inputs(d):
    bad = []; w = d["w"].astype(np.float64)
    if not np.isfinite(w).all() or (w < 0).any() or (w > 2.0 ** 20).any() or (np.sum(w, (0, 2)) < 1).any(): bad.append("w")
    p, c, e = [np.stack([gentries(a) for a in d[k]]) for k in ("pm", "cl", "en")]
    if (np.sort(p, -1) != np.arange(H)).any(): bad.append("pm")
    if (e < 0).any() or (e[..., -1] != H - 1).any() or (e[..., 1:] <= e[..., :-1]).any(): bad.append("en")
    if (c != classes(e)).any(): bad.append("cl")
    if (d["al"] < 0).any() or (d["al"] >= 2 ** M).any(): bad.append("al")
    if (d["tg"] < 0).any() or (d["tg"] > 1).any(): bad.append("tg")
    for k, lo, hi in (("st", 0.5, 1.0), ("ju", 0.0, JM), ("mi", 0.25, 1.0)):
        if not ((d[k] >= lo) & (d[k] <= hi)).all(): bad.append(k)
    return bad
def reference(w, pm, cl, en, al, tg, st, ju, mi):
    x = w.astype(np.float64).transpose(1, 0, 2).reshape(128, H); y = np.zeros((N, 128, H), np.float64)
    for r in range(N):
        x = np.take_along_axis(x, np.repeat(gentries(pm[r]), 16, 0), 1)
        a = np.repeat(np.take_along_axis(al[r], gentries(cl[r]), 1), 16, 0)
        for s in range(M):
            stay, jump, miss = [v[r][:, s:s + 1].astype(np.float64) for v in (st, ju, mi)]
            e = np.where(((a >> s) & 1) == tg[r][:, s:s + 1], 1.0, miss)
            x = e * (stay * x + jump * np.sum(x, 1, keepdims=True))
        y[r] = x
    return {"y": y.astype(np.float32)}

from concourse.bass import DstId, RemoteDMATransfer
from concourse.mybir import AluOpType as Alu, ActivationFunctionType as Act, AxisListType

F32, BF, I32, U16 = "float32", "bfloat16", "int32", "uint16"
SB = {
    "PI": (512, I32), "FI": (512, I32), "FB": (768, BF), "TF": (256, F32), "SL": (512, U16), "SLl": (512, U16),
    "ALi": (128, I32), "ALb": (128, BF), "TGi": (4, I32), "PO": (16, F32), "PR": (64, F32), "PC": (64, F32),
    "win": (4096, BF), "wrep": (4096, BF), "wfull": (4096, BF), "GB": (10 * 1024, BF), "JK": (3072, F32),
    "alw": (2048, BF), "CLu": (256, U16), "AF": (128, F32),
    "pcol": (4, I32), "pint": (4, I32), "pf": (4, F32), "D": (144, F32), "Base": (144, F32), "IA": (192, F32),
    "keep": (192, F32), "ident": (16, F32), "Wt": (16, F32), "WC": (8, F32), "Wd": (9 * 144, BF),
    "LCf": (64, F32), "LC": (128, U16), "BT": (448, F32), "Rep": (128, F32), "Red": (128, F32), "Blk": (128, F32),
    "Eb": (448, F32), "Fb": (448, F32), "JE": (448, F32), "PP": (128, F32), "TB": (128, F32), "Mv": (192, F32),
    "m1": (192, F32), "m2": (192, F32), "m3": (192, F32), "CN": (16, F32), "RN": (64, F32), "TC": (32, F32),
    "prod": (320, F32), "LS": (16 * 64, U16), "OUTL": (768, U16), "LL": (768, U16), "FL": (768, U16),
    "LT": (512, F32), "TO": (128, F32), "JT": (6 * 256, F32), "xs": (2064, F32), "xa": (1024, F32), "tt": (1032, F32),
    "JJ": (128, F32), "mi1": (256, I32), "mi2": (512, I32), "mf": (512, F32), "LM": (512, U16), "FX": (256, F32),
    "X": (4096, F32), "Z": (4096, F32),
}
SCRATCH = {k: ("sbuf", [128, v[0]], v[1]) for k, v in SB.items()}
SCRATCH.update({"wst": ("dram", [4, 128, 256], BF), "wl": ("dram", [4, 128, 256], BF), "fst": ("dram", [8, 128, 128], BF),
                "fl": ("dram", [6, 128, 128], BF), "sst": ("dram", [4, 128, 128], U16)})
SCRATCH.update({"ps%d" % b: ("psum", [128, 512], F32) for b in range(8)})
SEMAPHORES = ["qv", "qs", "qp", "qg", "sent", "rw", "rn", "rp", "rf", "rs", "rwf", "rA", "rL", "rB0", "rB1"] + ["d%d" % i for i in range(48)]
SEG = (0, 64, 128, 256)
NL = (0, 2, 2, 3)
ACC = True
BIAS = 0.5
CY, GA, HOP = 1.0e-3, 1.56, 0.15


def graph(g, T, topo, r):
    core = T.cores[r]
    others = [(r + d) % 4 for d in (1, 2, 3)]
    QQ = {"v": g.vector, "s": g.scalar, "p": g.tensor, "g": g, "y": g.sync}
    V, S = g.vector, g.scalar
    hist, waited, total, nd, nodes, seen = {}, {}, {}, [0], [], {}
    ne = len(topo.engines(core, T.cores[others[0]]))

    def R(name, c0, c1, p0=0, p1=128, step=1):
        ap = T[name][p0:p1, c0:c1] if step == 1 else T[name][p0:p1, c0:c1:step]
        if name.startswith("ps"):
            return (ap, name, 0, 512, 0, 128)
        return (ap, name, c0, c1, p0, p1)

    def RD(name, ap, s0, s1):
        return (ap, name, s0, s1, 0, 128)

    def IN(ap):
        return (ap, None, 0, 0, 0, 0)

    def clash(table, reads, writes):
        out = []
        for regs, wr in ((reads, False), (writes, True)):
            for x in regs:
                for (c0, c1, p0, p1, w, tok) in table.get(x[1], []):
                    if (w or wr or x[1].startswith("ps")) and c0 < x[3] and x[2] < c1 and p0 < x[5] and x[4] < p1:
                        out.append(tok)
        return out

    def note(table, reads, writes, tok):
        for regs, wr in ((reads, False), (writes, True)):
            for x in regs:
                if x[1] is not None:
                    table.setdefault(x[1], []).append((x[2], x[3], x[4], x[5], wr, tok))

    def wait(q, tok):
        if waited.get((q, tok[0]), 0) < tok[1]:
            QQ[q].wait_ge(T.sem[tok[0]], tok[1])
            waited[(q, tok[0])] = tok[1]

    def deps(q, reads, writes):
        need = {}
        for s, n in clash(hist, reads, writes):
            if not (q == "p" and s == "qp"):
                need[s] = max(need.get(s, 0), n)
        for k in need:
            wait(q, (k, need[k]))

    def issue(q, fn, reads, writes):
        deps(q, reads, writes)
        s = "q" + q
        total[s] = total.get(s, 0) + 1
        fn(q).then_inc(T.sem[s], 1)
        note(hist, reads, writes, (s, total[s]))

    def node(qs, cost, lat, reads, writes, emit, **kw):
        wr = [x for x in writes if x[1] != "JK"]
        n = dict(r=r, qs=qs, cost=cost, lat=lat, pre=set(clash(seen, reads, wr)), emit=emit, far=[], **kw)
        note(seen, reads, wr, len(nodes))
        nodes.append(n)

    def op(qs, cycles, fn, reads, writes):
        c = 0.06 + max(64, cycles) * CY
        node(qs, c, c, reads, writes, lambda q: issue(q, fn, reads, writes))

    def wid(x):
        return x[3] - x[2]

    def dmas(q, lst, kb, **kw):
        s = "d%d" % nd[0]
        nd[0] += 1

        def emit(q):
            total[s] = 16 * len(lst)
            for o, i in lst:
                deps(q, [i], [o])
                QQ[q].dma_start(o[0], i[0], **kw).then_inc(T.sem[s], 16)
            note(hist, [i for o, i in lst], [o for o, i in lst], (s, total[s]))
        node(q, (1.0 if q == "g" else 0.1) * len(lst), 2.0 + 0.1 * len(lst), [i for o, i in lst], [o for o, i in lst], emit, dma=kb / 250.0)

    def send(sem, trs, per, us, first=0):
        def emit(q):
            tl = []
            for n, (src, dsts) in enumerate(trs):
                deps("g", [src], [])
                es = topo.engines(core, T.cores[dsts[0][0]])
                es = es[0::2] + es[1::2]
                ids = [DstId(rid=topo.addr(T.cores[d])[0], pnc=topo.addr(T.cores[d])[1]) for d, _ in dsts]
                tl.append(RemoteDMATransfer(dst_ids=ids, dma_engine_mask=sum(1 << e for e in es[first + n * per:first + (n + 1) * per]),
                                            remote_sem=T.sem[sem], srcs=[src[0]], dsts=[a for _, a in dsts]))
                total["sent"] = total.get("sent", 0) + per
            g.remote_dma_fused(tl, local_sem=T.sem.sent)
        node("g", 0.6, 2.5 + us, [t[0] for t in trs], [], emit, sends=(sem, {d for t in trs for d, _ in t[1]}))

    def arrive(sem, n, regs):
        def emit(q):
            total[sem] = n
            note(hist, [], regs, (sem, n))
        node("", 0.0, 0.0, [], regs, emit, gets=sem)

    def ind(w, l):
        return w[0].indirect(l[0])

    def vcopy(o, i, qs="v"):
        op(qs, wid(o), lambda q: V.tensor_copy(o[0], i[0]) if q == "v" else S.activation(o[0], i[0], Act.Copy), [i], [o])

    def vts(o, i, s1, op0, s2=None, op1=None):
        rd = [i] + [x for x in (s1, s2) if isinstance(x, tuple)]
        a1 = s1[0] if isinstance(s1, tuple) else s1
        a2 = s2[0] if isinstance(s2, tuple) else s2
        tail = (None, op0) if op1 is None else (a2, op0, op1)
        op("v", wid(o), lambda q: V.tensor_scalar(o[0], i[0], a1, *tail), rd, [o])

    def vtt(o, a, b, alu, lst=None):
        if lst is None:
            op("v", 2 * wid(o), lambda q: V.tensor_tensor(o[0], a[0], b[0], alu), [a, b], [o])
        else:
            op("v", GA * wid(o), lambda q: V.tensor_tensor(o[0], ind(a, lst), b[0], alu), [a, b, lst], [o])

    def gather(qs, o, w, lst, acc=None):
        if acc is None:
            op(qs, GA * wid(o), lambda q: V.tensor_copy(o[0], ind(w, lst)) if q == "v" else S.activation(o[0], ind(w, lst), Act.Copy), [w, lst], [o])
        else:
            op("s", GA * wid(o), lambda q: S.activation(o[0], ind(w, lst), Act.Copy, accum_out=acc[0]), [w, lst], [o, acc])

    def scale(o, i, col, qs="s"):
        op(qs, wid(o), lambda q: S.activation(o[0], i[0], Act.Copy, scale=col[0]) if q == "s" else V.tensor_scalar(o[0], i[0], col[0], None, Alu.mult), [i, col], [o])

    def fill(x, val, n=64):
        op("v", n, lambda q: V.memset(x[0], val), [], [x])

    def iota(o, pat, base=0, cm=0):
        kw = {} if o[1] == "pcol" else {"allow_small_or_imprecise_dtypes": True}
        op("g", 130 + 2 * wid(o), lambda q: g.iota(o[0], pat, base, cm, **kw), [], [o])

    def chain(lst):
        for o, l, x, st, sp in lst:
            h = g.tensor.matmul(o[0], l[0], x[0], st, sp)
        return h

    def mms(lst):
        op("p", 256 * len(lst), lambda q: chain(lst), [m[1] for m in lst] + [m[2] for m in lst], [lst[0][0]])

    jk = [0]

    def junk():
        jk[0] += 1
        return R("JK", 1024 * (jk[0] % 3), 1024 * (jk[0] % 3) + 1024)

    dmas("y", [(R("PI", 0, 256), IN(T.pm[:, :]))], 128)
    dmas("s", [(R("PI", 256, 512), IN(T.cl[:, :]))], 128)
    dmas("y", [(R("ALi", 0, 128), IN(T.al[:, :]))], 64)
    dmas("s", [(R("PO", 0, 4), IN(T.st[:, :])), (R("PO", 4, 8), IN(T.ju[:, :])), (R("PO", 8, 12), IN(T.mi[:, :])), (R("TGi", 0, 4), IN(T.tg[:, :]))], 100)
    fill(R("alw", 0, 2048), 0.0, 1024)
    fill(R("win", 0, 4096), 0.0, 2048)

    iota(R("pcol", 0, 1), [[0, 1]], 0, 1)
    iota(R("D", 0, 144), [[1, 144]], 0, -1)
    iota(R("IA", 0, 192), [[0, 12], [1, 16]])
    iota(R("LCf", 0, 16), [[1, 16]])
    iota(R("LCf", 16, 20), [[16, 4]], 0)
    iota(R("LCf", 20, 24), [[16, 4]], 1)
    iota(R("LCf", 24, 32), [[0, 2], [16, 4]], 2)
    iota(R("LCf", 32, 44), [[0, 3], [16, 4]], 3)
    iota(R("Rep", 0, 128), [[0, 4], [-1, 32]], -32 * r, 1)
    iota(R("BT", 0, 64), [[0, 32], [1, 2]])
    iota(R("BT", 64, 128), [[0, 16], [1, 2], [0, 2]])
    iota(R("BT", 128, 256), [[0, 16], [1, 2], [0, 4]])
    iota(R("BT", 256, 448), [[0, 12], [1, 2], [0, 8]])
    iota(R("Red", 0, 128), [[0, 4], [1, 32]])
    iota(R("Blk", 0, 128), [[0, 4], [1, 2], [0, 16]], 2 * r)
    iota(R("JJ", 0, 128), [[0, 2], [16, 64]], -1024)
    vts(R("pint", 0, 1), R("pcol", 0, 1), 15, Alu.bitwise_and)
    vts(R("pint", 1, 2), R("pcol", 0, 1), 31, Alu.bitwise_and)
    vts(R("pint", 2, 3), R("pcol", 0, 1), 4, Alu.arith_shift_right)
    vcopy(R("pf", 0, 3), R("pint", 0, 3))
    vts(R("pf", 3, 4), R("pf", 0, 1), -1.0, Alu.mult, 16.0, Alu.add)
    vts(R("Base", 0, 144), R("D", 0, 144), R("pf", 3, 4), Alu.is_equal)
    vts(R("ident", 0, 16), R("IA", 0, 16), R("pf", 0, 1), Alu.is_equal)
    for c0, c1, st, val in ((0, 16, 1, 1.0), (4, 12, 4, 256.0), (1, 2, 1, 16.0)):
        fill(R("Wt", c0, c1, step=st), val)
    vtt(R("Wt", 0, 16), R("Wt", 0, 16), R("ident", 0, 16), Alu.mult)
    vtt(R("WC", 0, 3), R("Wt", 0, 12, step=4), R("Wt", 1, 12, step=4), Alu.add)
    vts(R("WC", 6, 8), R("ident", 2, 16, step=8), 16.0, Alu.mult)
    TY = {"c0": ("WC", 0), "c1": ("WC", 1), "c2": ("WC", 2), "b0": ("WC", 6), "b2": ("WC", 7),
          "a0": ("ident", 2), "a1": ("ident", 6), "a2": ("ident", 10), "z": ("ident", 0)}
    tyc = {}
    for n, k in enumerate(TY):
        tyc[k] = 144 * n
        scale(R("Wd", 144 * n, 144 * n + 144), R("Base", 0, 144), R(TY[k][0], TY[k][1], TY[k][1] + 1), "sv")
    Lhi, Llo, Lsq, Lsq4 = R("LC", 0, 16), R("LC", 16, 32), R("LC", 32, 60), R("LC", 64, 92)
    vcopy(Lhi, R("LCf", 0, 16))
    vts(Llo, R("LCf", 0, 16), 0.0, Alu.mult, R("pf", 0, 1), Alu.add)
    vcopy(Lsq, R("LCf", 16, 44))
    vts(Lsq4, R("LCf", 16, 44), 4.0, Alu.add)
    vts(R("LC", 96, 108), R("LCf", 0, 12), 16.0, Alu.mult, 15.0, Alu.add)
    LX = [R("LC", 108 + 4 * n, 112 + 4 * n) for n in range(3)]
    for n, c in enumerate((0.0, 1.0, 4.0)):
        vts(LX[n], R("LCf", 0, 4), 16.0, Alu.mult, c, Alu.add)
    vts(R("JJ", 0, 128), R("JJ", 0, 128), R("pf", 0, 1), Alu.add)
    for x in (R("xs", 1024, 1032), R("xs", 2056, 2064), R("tt", 1024, 1032)):
        fill(x, 0.0)
    vts(R("Rep", 0, 128), R("Rep", 0, 128), 0.0, Alu.is_equal)
    vts(R("keep", 0, 192), R("IA", 0, 192), 1.0, Alu.min)
    vts(R("Red", 0, 128), R("Red", 0, 128), R("pf", 1, 2), Alu.is_equal)
    vts(R("Blk", 0, 128), R("Blk", 0, 128), R("pf", 2, 3), Alu.is_equal)

    slot, bank, pend, lists = {}, [0], {}, {}
    for q in range(4):
        lists["c%d%d" % (q, q)] = R("SLl", 128 * q, 128 * q + 64)
        lists["a%d%d" % (q, q)] = R("SLl", 128 * q + 64, 128 * q + 128)
    for o in (1, 2, 3):
        lists["c%d0" % o] = R("OUTL", 192 * o, 192 * o + 64)
        lists["j%d0" % o] = R("OUTL", 192 * o + 64, 192 * o + 128)
    lists["j32"] = R("OUTL", 704, 768)
    nls = [0]

    def G(name):
        return slot.setdefault(name, 1024 * len(slot))

    def L(name):
        if name not in lists:
            lists[name] = R("LS", 64 * nls[0], 64 * nls[0] + 64)
            nls[0] += 1
        return lists[name]

    def halves(name, c, w, l):
        for h in (0, 1):
            gather("sv", R(name, c + 512 * h, c + 512 * h + 512), w, R(l[1], l[2] + 32 * h, l[2] + 32 * h + 32))

    def wrap(name, parts, outs, plus=None):
        virt = (None, "w" + name, 0, 1, 0, 128)
        rd = [R("Wd", tyc[ty], tyc[ty] + 144) for ty, src in parts] + [R("GB", G(src), G(src) + 1024) for ty, src in parts]

        def emit(q):
            b = bank[0]
            bank[0] += 1
            ps = pend[name] = R("ps%d" % (b % 6), 64 * (b // 6), 64 * (b // 6) + 64)
            ml = [[ps, R("Wd", tyc[ty] + 16 - i, tyc[ty] + 144 - i), R("GB", G(src) + i, G(src) + 1024, step=16), False, False]
                  for ty, src in parts for i in range(16)]
            ml[0][3] = True
            ml[-1][4] = True
            issue("p", lambda q: chain(ml), rd, [ps])
        c = 1024 * len(parts) * CY
        node("p", c, c, rd, [virt], emit)
        for o in outs:
            if plus is None:
                node("v", 0.13, 0.13, [virt], [o], lambda q, o=o: issue("v", lambda q: V.tensor_copy(o[0], pend[name][0]), [pend[name]], [o]))
            else:
                node("v", 0.13, 0.13, [virt, plus], [plus], lambda q: issue("v", lambda q: V.tensor_tensor(plus[0], pend[name][0], plus[0], Alu.add), [pend[name], plus], [plus]))
                vcopy(o, plus)

    def masks(q):
        c, a = 128 * q, R("mi1", 64 * q, 64 * q + 64)
        vts(R("mi2", c, c + 64), a, 1, Alu.bitwise_and)
        vts(R("mi2", c + 64, c + 128), a, 2, Alu.arith_shift_right, 1, Alu.bitwise_and)
        vtt(R("mf", c, c + 128), R("mi2", c, c + 128), R("JJ", 0, 128), Alu.mult)
        vts(R("LM", c, c + 128), R("mf", c, c + 128), 1024.0, Alu.add)

    vcopy(R("ALb", 0, 128), R("ALi", 0, 128))
    alb = len(nodes) - 1
    for e in (0, 1):
        dmas("ys"[e], [(R("alw", 0, 2048, 16 * c, 16 * c + 1), R("ALb", 0, 128, 16 * c, 16 * c + 16)) for c in range(4 * e, 4 * e + 4)], 20)
    dmas("y", [(RD("wst", T.wst[:], 0, 4), IN(T.w[:, :]))], 256)
    nodes[-1]["pre"].add(alb)
    dmas("y", [(R("wfull", 1024 * r, 1024 * r + 1024), IN(T.w[:, :]))], 256)
    nodes[-1]["pre"].add(alb)
    vcopy(R("CLu", 0, 256), R("PI", 256, 512))
    vts(R("FI", 0, 256), R("PI", 0, 256), 15, Alu.bitwise_and)
    vts(R("FI", 256, 512), R("PI", 0, 256), 4, Alu.arith_shift_right)
    for k in range(4):
        halves("GB", G("z%d" % k), R("alw", 0, 2048), R("CLu", 64 * k, 64 * k + 64))
        wrap("z%d" % k, [("z", "z%d" % k)], [R("SL", 256 + 64 * k, 320 + 64 * k)] + ([R("FB", 512 + 64 * k, 576 + 64 * k)] if r < 3 else []))
    if r < 3:
        vcopy(R("FB", 0, 512), R("FI", 0, 512))
        dmas("y", [(RD("fst", T.fst[:, 32 * e:32 * e + 32, :], e, e + 1), R("FB", 256 * f, 256 * f + 256)) for e, f in ((0, 0), (1, 1), (3, 0))], 200)
        dmas("y", [(RD("fst", T.fst[:, 64:96, :], 2, 3), R("FB", 512, 768))], 70)
    if r == 0:
        vcopy(R("SL", 0, 256), R("PI", 0, 256))
    else:
        vts(R("TF", 0, 256), R("FI", 0, 256), 256.0, Alu.mult)
        vtt(R("TF", 0, 256), R("TF", 0, 256), R("FI", 256, 512), Alu.add)
        vcopy(R("SL", 0, 256), R("TF", 0, 256))
    for l in (0, 1):
        dmas("y", [(RD("sst", T.sst[:, 32 * k:32 * k + 32, 64 * l:64 * l + 64], 4 * l + k, 4 * l + k + 1),
                    R("SL", 256 * l + 64 * k, 256 * l + 64 * k + 64)) for k in range(4)], 200)
    fill(R("CN", 4 * r, 4 * r + 4), 0.0)
    gather("s", R("Z", 0, 4096), R("ident", 0, 16), R("SL", 256, 512), R("CN", 4 * r, 4 * r + 1))
    send("rn", [(R("CN", 4 * r, 4 * r + 4), [(d, T.CN[:, 4 * r:4 * r + 4]) for d in others])], ne // 2, 2.0)
    arrive("rn", 3 * (ne // 2), [R("CN", 4 * q, 4 * q + 4) for q in others])
    for q in range(4):
        scale(R("RN", 16 * q, 16 * q + 16), R("ident", 0, 16), R("CN", 4 * q, 4 * q + 1), "sv")
    vcopy(R("PO", 12, 16), R("TGi", 0, 4))
    vcopy(R("PR", 16 * r, 16 * r + 16), R("PO", 0, 16))
    send("rp", [(R("PO", 0, 16), [(d, T.PR[:, 16 * r:16 * r + 16]) for d in others])], ne, 2.0)
    arrive("rp", 3 * ne, [R("PR", 16 * q, 16 * q + 16) for q in others])
    if r < 3:
        send("rf", [(RD("fst", T.fst[2 * d + h], 0, 8), [(d, T.fl[3 * h + r])]) for d in others for h in (0, 1)], 1, 3.0)
        dmas("y", [(RD("fl", T.fl[3 * h + r], 3 * h + r, 3 * h + r + 1), RD("fst", T.fst[2 * r + h], 0, 8)) for h in (0, 1)], 64)
    fsrc = [q for q in others if q < 3]
    arrive("rf", 2 * len(fsrc), [RD("fl", None, 3 * h + q, 3 * h + q + 1) for q in fsrc for h in (0, 1)])
    send("rs", [(RD("sst", T.sst[d], 0, 8), [(d, T.SLl[:, 128 * r:128 * r + 128])]) for d in others], ne // 4, 3.0)
    arrive("rs", 3 * (ne // 4), [R("SLl", 128 * q, 128 * q + 128) for q in others])
    dmas("y", [(R("SLl", 128 * r, 128 * r + 128), RD("sst", T.sst[r], 0, 8))], 60)
    send("rw", [(RD("wst", T.wst[d], d, d + 1), [(d, T.wl[r])]) for d in others], ne // 4, 4.0)
    arrive("rw", 3 * (ne // 4), [RD("wl", None, 0, 4)])
    send("rwf", [(R("wfull", 1024 * r, 1024 * r + 1024), [(d, T.wfull[:, 1024 * r:1024 * r + 1024]) for d in others])], ne // 2, 22.0, ne // 2)
    nodes[-1]["pre"] |= {i for i, n in enumerate(nodes) if n.get("sends", ("",))[0] in ("rf", "rs")}
    arrive("rwf", 3 * (ne // 2), [R("wfull", 1024 * q, 1024 * q + 1024) for q in others])
    for e in (0, 1):
        dmas("y", [(R("win", 0, 4096, 32 * k + 16 * h, 32 * k + 16 * h + 12), RD("fl", T.fl[3 * h:3 * h + 3], 3 * h, 3 * h + 3))
                   for k in (2 * e, 2 * e + 1) for h in (0, 1)], 384)
    dmas("y", [(R("wrep", 1024 * q, 1024 * q + 1024, 32 * k, 32 * k + 32),
                IN(T.w[32 * r:32 * r + 32, :]) if q == r else RD("wl", T.wl[q], q, q + 1)) for q in [r] + others for k in range(4)], 1024)

    mms([(R("ps7", 0, 64), R("Rep", 0, 128), R("PR", 0, 64), True, True)])
    vcopy(R("PC", 0, 64), R("ps7", 0, 64))
    vtt(R("Eb", 0, 448), R("PC", 8, 64), R("BT", 0, 448), Alu.is_equal, Lsq4)
    vtt(R("Eb", 0, 448), R("PC", 8, 64), R("Eb", 0, 448), Alu.max, Lsq)
    vtt(R("Fb", 0, 448), R("PC", 0, 64), R("Eb", 0, 448), Alu.mult, Lsq)
    vtt(R("JE", 0, 448), R("PC", 0, 64), R("Eb", 0, 448), Alu.mult, Lsq4)
    vtt(R("PP", 0, 64), R("Fb", 0, 64), R("Fb", 64, 128), Alu.mult)
    vtt(R("PP", 64, 128), R("PP", 0, 64), R("Fb", 128, 192), Alu.mult)
    vtt(R("TB", 0, 64), R("PP", 64, 128), R("Fb", 256, 320), Alu.mult)
    vcopy(R("Mv", 0, 192), R("JE", 0, 192), "sv")
    gather("sv", R("FX", 0, 64), R("Fb", 0, 64), LX[0])
    gather("sv", R("FX", 128, 192), R("Fb", 128, 192), LX[0])
    vtt(R("FX", 64, 128), R("Fb", 0, 64), R("FX", 0, 64), Alu.subtract, LX[1])
    vtt(R("FX", 192, 256), R("Fb", 128, 192), R("FX", 128, 192), Alu.subtract, LX[2])
    vtt(R("FX", 128, 192), R("FX", 128, 192), R("JE", 256, 320), Alu.mult)
    vtt(R("FX", 192, 256), R("FX", 192, 256), R("JE", 256, 320), Alu.mult)
    send("rA", [(R("TB", 0, 64), [(d, T.LT[:, 128 * r:128 * r + 64]) for d in others])], ne // 2, 3.0)
    arrive("rA", 3 * (ne // 2), [R("LT", 128 * q, 128 * q + 64) for q in others])

    vcopy(R("mi1", 192, 256), L("a33"))
    masks(3)
    vcopy(R("AF", 0, 64), L("a11"))
    vcopy(R("AF", 64, 128), L("a33"))
    for o in (3, 2, 1):
        for q in range(o - 1, -1, -1):
            n = "%d%d" % (o, q)
            halves("GB", G("s" + n), R("win", 0, 4096), L("c%d%d" % (o, q + 1)))
            wrap("c" + n, [("c%d" % q, "s" + n)], [L("c" + n)])
            if o == 3:
                wrap("a" + n, [("a%d" % q, "s" + n)], [L("a" + n), R("mi1", 64 * q, 64 * q + 64)])
                masks(q)
            if q % 2 == 0 and q + 1 == o:
                wrap("j" + n, [("b%d" % q, "s" + n)], [L("j" + n)], R("AF", 32 * q, 32 * q + 64))
            elif q == 0:
                wrap("j" + n, [("b0", "s" + n), ("a1", "s%d1" % o)], [L("j" + n)])
        w = 64 * NL[o]
        if o != r:
            send("rL", [(R("OUTL", 192 * o, 192 * o + w), [(o, T.LL[:, 192 * r:192 * r + w])])], ne // 2, 3.0)

    mms([(R("ps7", 64 * t, 64 * t + 64), R("Blk", 0, 128), R("RN", 0, 64), True, True) for t in range(3)])
    for u in (1, 2, 3):
        w = 64 * u
        op("v", w, lambda q, w=w: V.tensor_tensor(T.m1[:, 0:w], T.ps7[:, 0:w], T.Mv[:, 0:w], Alu.mult), [R("ps7", 0, w), R("Mv", 0, w)], [R("m1", 0, w)])
        vtt(R("m3", 0, w), R("Fb", SEG[u], SEG[u] + w), R("Mv", 0, w), Alu.mult)
        op("v", w, lambda q, w=w: V.tensor_tensor_scan(T.m2[:, 0:w], T.keep[:, 0:w], T.m1[:, 0:w], 0.0, Alu.mult, Alu.add),
           [R("keep", 0, w), R("m1", 0, w)], [R("m2", 0, w)])
        vtt(R("m1", 0, w), R("m2", 0, w), R("JE", SEG[u], SEG[u] + w), Alu.mult, R("LC", 96, 96 + 4 * u))
        vtt(R("Mv", 0, w), R("m1", 0, w), R("m3", 0, w), Alu.add)
    vtt(R("FX", 0, 64), R("FX", 0, 64), R("Mv", 64, 128), Alu.mult)
    vtt(R("Mv", 64, 128), R("FX", 64, 128), R("Mv", 64, 128), Alu.mult)
    vtt(R("Mv", 128, 192), R("FX", 128, 192), R("Mv", 128, 192), Alu.add)
    vtt(R("Mv", 0, 64), R("FX", 0, 64), R("Mv", 0, 64), Alu.add)

    made = {}
    for q in range(4):
        c0 = 1032 * (q % 2)
        x, a = R("xs", c0, c0 + 1024), L("a3%d" % q)
        col = [R("TC", 8 * q + s, 8 * q + s + 1) for s in range(4)]
        if q == 0:
            halves("xs", 0, R("wrep", 0, 4096), L("c30"))
        else:
            vtt(x, R("TB", 48 + 16 * q, 64 + 16 * q), R("xa", 0, 1024), Alu.add, L("a3%d" % (q - 1)))
        vtt(R("tt", 0, 1024), R("PP", 16 * q, 16 * q + 16), x, Alu.mult, a)
        for s in range(4):
            if s % 2:
                gather("s", junk(), R("xs", c0, c0 + 1032) if s == 1 else R("tt", 0, 1032), R("LM", 128 * q + 32 * s - 32, 128 * q + 32 * s + 32), col[s])
            else:
                i, o = (x if s == 0 else R("tt", 0, 1024)), junk()
                op("sv", 1024, lambda e, i=i, o=o, c=col[s]: S.activation(o[0], i[0], Act.Copy, accum_out=c[0]) if e == "s"
                   else V.tensor_reduce(c[0], i[0], AxisListType.X, Alu.add), [i], [o, col[s]])
            if q and s > 1:
                nodes[-1]["pre"].add(made[s - 2])
            m = R("FX", 192 + 16 * q, 208 + 16 * q) if s == 3 else R("Mv", 64 * s + 16 * q, 64 * s + 16 * q + 16)
            pr = R("prod", 64 * q + 16 * s, 64 * q + 16 * s + 16)
            scale(pr, m, col[s])
            made[s] = len(nodes) - 1
            mms([(R("ps6", 0, 16), R("Red", 0, 128), pr, s == 0, s == 3)])
        vcopy(R("TB", 64 + 16 * q, 80 + 16 * q), R("ps6", 0, 16))
        if q < 3:
            vtt(R("xa", 0, 1024), R("TB", 16 * q, 16 * q + 16), x, Alu.mult, a)
        b0, b1, dst, sem = ((64, 80, [0], "rB0"), (64, 96, [1, 2, 3], "rB0"), (96, 112, [2], "rB1"), (96, 128, [3], "rB1"))[q]
        dst = [d for d in others if d in dst]
        if dst:
            send(sem, [(R("TB", b0, b1), [(d, T.LT[:, 128 * r + b0:128 * r + b1]) for d in dst])], ne, 0.7 * len(dst))

    def mine(c0, c1):
        for c in [r] + others:
            src = R("TB", c0, c1, 32 * c, 32 * c + 32) if c == r else R("LT", 128 * c + c0, 128 * c + c1, 32 * c, 32 * c + 32)
            vcopy(R("TO", c0, c1, 32 * c, 32 * c + 32), src, "sv")

    mine(0, 64)
    w = 64 * NL[r]
    if r:
        arrive("rL", 3 * (ne // 2), [R("LL", 192 * c, 192 * c + w) for c in others])
        dmas("y", [(R("FL", 192 * k, 192 * k + w, 32 * c, 32 * c + 32),
                    R("OUTL", 192 * r, 192 * r + w, 32 * k, 32 * k + 32) if c == r else R("LL", 192 * c, 192 * c + w, 32 * k, 32 * k + 32))
                   for c in [r] + others for k in range(4)], 300)

    def fl(l, k, a=0, b=64):
        if l >= NL[r]:
            c = 64 * k + (256 if l else 0)
            return R("SL", c + a, c + b)
        return R("FL", 192 * k + 64 * l + a, 192 * k + 64 * l + b)

    for k in range(4):
        halves("X", 1024 * k, R("wfull", 0, 4096), fl(0, k))
    soft = []
    for j in range(1 + r // 2):
        b0, b1 = 64 + 32 * j, 80 + 32 * j + 16 * (r % 2 if j == r // 2 else 1)
        arrive("rB%d" % j, 3 * ne, [R("LT", 128 * c + b0, 128 * c + b1) for c in others])
        mine(b0, b1)
        tA, tB = R("TO", 32 * j, 32 * j + 16), R("TO", b0, b0 + 16)
        if b1 - b0 == 32:
            A1, jA, jB = [R("JT", 768 * j + 256 * n, 768 * j + 256 * n + 256) for n in range(3)]
            gather("sv", A1, R("TO", 32 * j + 16, 32 * j + 32), Llo)
            vtt(jA, tA, A1, Alu.mult, Lhi)
            vtt(jB, tB, A1, Alu.mult, Lhi)
            vtt(jB, R("TO", b0 + 16, b0 + 32), jB, Alu.add, Llo)
            tA, tB = jA, jB
        for k in range(8):
            x, l = R("X", 512 * k, 512 * k + 512), fl(1 + j, k // 2, 32 * (k % 2), 32 * (k % 2) + 32)
            vtt(x, tA, x, Alu.mult, l)
            soft.append(len(nodes) - 1)
            if j < r // 2 and ACC:
                gather("s", R("Z", 512 * k, 512 * k + 512), tB, l)
                if k % 2:
                    dmas("g", [(R("X", 512 * k - 512, 512 * k + 512), R("Z", 512 * k - 512, 512 * k + 512))], 1024, accum_op=Alu.add)
            else:
                vtt(x, tB, x, Alu.add, l)
                soft.append(len(nodes) - 1)
            if j == r // 2:
                dmas("y", [(IN(T.y[:, 512 * k:512 * k + 512]), x)], 256)
    for a, b in zip(soft, soft[1:]):
        nodes[a]["far"].append(b)

    def finish():
        for s in total:
            if max([waited.get((q, s), 0) for q in QQ]) < total[s]:
                wait("y", (s, total[s]))
    return nodes, finish


def schedule(graphs):
    alln = []
    for nodes in graphs:
        base = len(alln)
        for n in nodes:
            n["pre"] = [base + i for i in n["pre"]]
            n["far"] = [base + i for i in n["far"]]
        alln += nodes
    for n in alln:
        if "gets" in n:
            n["pre"] += [i for i, m in enumerate(alln) if "sends" in m and m["sends"][0] == n["gets"] and n["r"] in m["sends"][1]]
    succ = [list(n["far"]) for n in alln]
    for i, n in enumerate(alln):
        for p in n["pre"]:
            succ[p].append(i)
    rank = {}

    def up(i):
        if i not in rank:
            n = alln[i]
            rank[i] = n["lat"] + n.get("dma", 0.0) + HOP + max([up(j) for j in succ[i]] + [0.0])
        return rank[i]

    def gap(lst, t, c):
        for a, b in lst:
            if t + c <= a:
                break
            t = max(t, b)
        return t

    busy = {}
    for i in sorted(range(len(alln)), key=lambda i: -up(i)):
        n = alln[i]
        t0 = max([alln[p]["end"] + (HOP if n["qs"] else 0.0) for p in n["pre"]] + [0.0])
        if not n["qs"]:
            n["at"], n["q"], n["end"] = t0, "", t0
            continue
        t, k, q = min((gap(busy.setdefault((n["r"], q), []), t0, n["cost"]) + k * BIAS, k, q) for k, q in enumerate(n["qs"]))
        t -= k * BIAS
        n["at"], n["q"], n["end"] = t, q, t + n["lat"]
        busy[(n["r"], q)].append((t, t + n["cost"]))
        busy[(n["r"], q)].sort()
        if "dma" in n:
            lst = busy.setdefault((n["r"], "dma"), [])
            d = gap(lst, t + 1.5, n["dma"])
            lst.append((d, d + n["dma"]))
            lst.sort()
            n["end"] = max(n["end"], d + n["dma"] + 0.5)


def rank_program(g, core, T, topo):
    r = T.rank_of(core)
    if r is None:
        return
    graphs = [graph(g, T, topo, q) for q in range(4)]
    schedule([x[0] for x in graphs])
    nodes, finish = graphs[r]
    for k in sorted(range(len(nodes)), key=lambda k: (nodes[k]["at"], k)):
        nodes[k]["emit"](nodes[k]["q"])
    finish()
